import numpy as np
import ml_dtypes


def mxq(x, axis, fmt="e4m3"):
    dtype, down = {"e4m3": (ml_dtypes.float8_e4m3fn, 7), "e5m2": (ml_dtypes.float8_e5m2, 14)}[fmt]
    v = np.moveaxis(np.asarray(x, np.float32).astype(ml_dtypes.bfloat16).astype(np.float64), axis, -1)
    blocks = v.reshape(v.shape[:-1] + (-1, 32))
    amax = np.abs(blocks).max(-1, keepdims=True)
    byte = np.maximum(np.where(amax > 0, np.frexp(amax)[1] - 1 + 127, 0) - down, 1)
    scale = np.exp2(byte - 127.0)
    codes = (blocks / scale).astype(np.float32).astype(dtype).astype(np.float64)
    return np.moveaxis((codes * scale).reshape(v.shape), -1, axis)


WIDE = False


def mx_kscale(k):
    if not WIDE:
        return np.ones(k)
    levels = np.array([10, -10, 5, -5, 0])
    if k % 512:
        return np.exp2(np.random.permutation(np.resize(levels, k // 32))).repeat(32)
    a = np.empty((k // 512, 16))
    for p in range(k // 512):
        a[p, :8] = np.random.permutation(np.resize(levels, 8))
        for g in range(8):
            far = levels[np.abs(levels - a[p, g]) >= 10]
            a[p, g + 8] = far[np.random.randint(len(far))]
    return np.exp2(a.ravel()).repeat(32)


def f64(x):
    return np.asarray(x).astype(np.float64)


def striped(idx):
    return np.tile(np.asarray(idx).reshape(-1, 16).T, (8, 1)).astype(np.uint16)


def unstriped(offs):
    return offs[:16].T.reshape(-1).astype(np.int64)


E2M1 = np.array([0.0, 0.5, 1.0, 1.5, 2.0, 3.0, 4.0, 6.0, -0.0, -0.5, -1.0, -1.5, -2.0, -3.0, -4.0, -6.0])


def pack_weight(w, fmt):
    k, n = w.shape
    w = f64(np.asarray(w, np.float32).astype(ml_dtypes.bfloat16)).reshape(k // 32, 32, n)
    amax = np.abs(w).max(1)
    if fmt == "e4m3":
        byte = np.frexp(amax)[1] - 1 + 127 - 7
    else:
        mant, ex = np.frexp(amax / 6.0)
        byte = np.where(mant > 0.5, ex, ex - 1) + 127
    byte = np.clip(np.where(amax > 0, byte, 1), 1, 254)
    scaled = (w * np.exp2(127.0 - byte)[:, None, :]).reshape(k, n).astype(np.float32)
    by_word = np.ascontiguousarray(scaled.reshape(k // 512, 128, 4, n).transpose(0, 1, 3, 2))
    if fmt == "e4m3":
        words = by_word.astype(ml_dtypes.float8_e4m3fn).view(np.uint8)
    else:
        c = by_word.astype(ml_dtypes.float4_e2m1fn).view(np.uint8) & 0xF
        words = (c[..., 0::2] | (c[..., 1::2] << 4)).reshape(k // 512, 128, 2 * n)
    return np.ascontiguousarray(words), np.ascontiguousarray(byte.astype(np.uint8).reshape(k // 512, 16, n))


def unpack_weight(words, scales, fmt):
    g, _, n = scales.shape
    words = np.ascontiguousarray(words).reshape(g, 128, n, -1)
    if fmt == "e4m3":
        vals = words.view(ml_dtypes.float8_e4m3fn).astype(np.float64)
    else:
        nib = np.empty((g, 128, n, 4), np.uint8)
        nib[..., 0::2] = words & 0xF
        nib[..., 1::2] = words >> 4
        vals = E2M1[nib]
    vals = vals * np.repeat(np.exp2(scales.astype(np.float64) - 127.0), 8, axis=1)[..., None]
    return vals.transpose(0, 1, 3, 2).reshape(g * 512, n)


D, E, T, I, Q = 512, 512, 1024, 256, 512


def setup_inputs():
    n = np.random.standard_normal
    idx = np.random.permutation(T)[:I]
    fd = mx_kscale(D)
    fq = mx_kscale(Q)
    keysp = pack_weight(n((D, T)) / fd[:, None], "e2m1")
    return {
        "query": (n((D, Q)) * 1.0 / np.sqrt(D) * fd[:, None]).astype(np.float32),
        "keys_words": keysp[0],
        "keys_scales": keysp[1],
        "sharp": (np.random.uniform(0.4, 1.0, (Q, 1))).astype(np.float32),
        "qs": (np.random.uniform(2.0, 8.0, (Q, 1)) * fq[:, None]).astype(np.float32),
        "grows": (n((Q, E)) / fq[:, None]).astype(np.float32),
        "old": (n((E, T)) * 2.0).astype(np.float32),
        "fade": (np.random.uniform(0.5, 1.0, (1, T))).astype(np.float32),
        "offs": striped(idx),
    }


def reference(query, keys_words, keys_scales, sharp, qs, grows, old, fade, offs):
    idx = unstriped(offs)
    keysu = unpack_weight(keys_words, keys_scales, "e2m1")
    queryq = mxq(f64(query), 0, "e4m3")
    keysidxg = keysu[:, idx]
    a = queryq.T @ keysidxg
    m1 = np.mean(a, axis=1, keepdims=True)
    ce = a - m1
    sd = np.sqrt(np.mean(np.square(ce), axis=1, keepdims=True) + 0.05)
    s = ce / sd * f64(sharp)
    p = np.exp(s - np.max(s, axis=1, keepdims=True))
    z = np.sum(p, axis=1, keepdims=True)
    w = p / z
    wq = w * f64(qs)
    growsq = mxq(f64(grows), 0, "e4m3")
    wqq = mxq(wq, 0, "e4m3")
    gv = growsq.T @ wqq
    gf = np.zeros((E, T))
    gf[:, idx] = gv
    y = f64(old) * f64(fade) + gf
    return y

@@ -1,0 +1,226 @@
+from contextlib import ExitStack
+
+import concourse.mybir as mybir
+from concourse.masks import make_identity
+
+D, E, T, I, Q = 512, 512, 1024, 256, 512
+FLOPS = 2 * D * Q * I + 2 * Q * E * I
+
+F32 = mybir.dt.float32
+BF16 = mybir.dt.bfloat16
+I32 = mybir.dt.int32
+U32 = mybir.dt.uint32
+U16 = mybir.dt.uint16
+U8 = mybir.dt.uint8
+FP8X4 = mybir.dt.float8_e4m3fn_x4
+FP4X4 = mybir.dt.float4_e2m1fn_x4
+ALU = mybir.AluOpType
+ACT = mybir.ActivationFunctionType
+
+P = 128
+PACK = 4
+EPS = 0.05
+HALF_T = T // 2
+HALF_I = I // 2
+
+
+def tile_attend_bstandardised_v_kernel(tc, query, keys_words, keys_scales, sharp, qs, grows, old, fade, offs, out):
+    nc = tc.nc
+    with ExitStack() as ctx:
+        sb = ctx.enter_context(tc.tile_pool(name="sb", bufs=1))
+        ps = ctx.enter_context(tc.psum_pool(name="ps", bufs=1))
+
+        def bank(tag, name):
+            return ps.tile([P, 512], F32, tag=tag, name=name)
+
+        offsets = sb.tile([P, I // 16], U16, name="offsets")
+        nc.sync.dma_start(offsets[:], offs)
+        key_scale_pool = sb.tile([P, T], U8, name="key_scale_pool", tag="slot_b", align_bytes=64)
+        nc.gpsimd.memset(key_scale_pool[:].bitcast(I32), 0)
+        for quad in range(4):
+            nc.scalar.dma_start(key_scale_pool[32 * quad : 32 * quad + 4, :].bitcast(I32),
+                                keys_scales[0, 4 * quad : 4 * quad + 4, :].bitcast(I32))
+        key_word_pool = sb.tile([P, T], U16, name="key_word_pool", tag="slot_a", align_bytes=64)
+        nc.sync.dma_start(key_word_pool[:].bitcast(I32), keys_words[0].bitcast(I32))
+
+        query_rows = query.rearrange("(p t) q -> p t q", t=PACK)
+        query_raw = []
+        for u in range(2):
+            raw = sb.tile([P, PACK, Q // 2], F32, name=f"query_raw{u}", tag=f"slot_q{u}", align_bytes=64)
+            nc.sync.dma_start(raw[:], query_rows[:, :, u * (Q // 2) : (u + 1) * (Q // 2)])
+            query_raw.append(raw)
+        ident = sb.tile([P, P], F32, name="ident")
+        make_identity(nc, ident[:])
+        sharp_sb = sb.tile([P, PACK], F32, name="sharp_sb")
+        nc.gpsimd.dma_start(sharp_sb[:], sharp.rearrange("(p r) o -> p (r o)", r=PACK))
+        qs_sb = sb.tile([P, PACK], F32, name="qs_sb")
+        nc.gpsimd.dma_start(qs_sb[:], qs.rearrange("(p r) o -> p (r o)", r=PACK))
+        minus_half = sb.tile([P, 2], F32, name="minus_half")
+        nc.gpsimd.memset(minus_half[:], -0.5)
+
+        windows = []
+        for k in range(4):
+            window = sb.tile([P, T], F32, name=f"window{k}")
+            nc.vector.memset(window[:].bitcast(I32), 0)
+            windows.append(window)
+            if k == 1:
+                fade_rows = sb.tile([P, P], F32, name="fade_rows")
+                nc.vector.memset(fade_rows[:], 0.0)
+                nc.scalar.dma_start(fade_rows[0:8, :], fade.rearrange("o (c n) -> (o c) n", n=P))
+
+
+        key_words = sb.tile([P, I], U16, name="key_words", align_bytes=64)
+        nc.vector.tensor_copy(key_words[:], key_word_pool[:].indirect(offsets[:]))
+
+        query_bf = sb.tile([P, PACK, P, PACK], BF16, name="query_bf", align_bytes=64)
+        for u in range(2):
+            nc.vector.tensor_copy(query_bf[:, :, u * (P // 2) : (u + 1) * (P // 2), :].rearrange("p r s t -> p s t r"),
+                                  query_raw[u][:].rearrange("p t (s r) -> p s t r", r=PACK))
+            if u == 0:
+                key_scales = sb.tile([P, I], U8, name="key_scales", align_bytes=64)
+                nc.vector.tensor_copy(key_scales[:], key_scale_pool[:].indirect(offsets[:]))
+        grows_raw = sb.tile([P, PACK, E], F32, name="grows_raw", tag="slot_a", align_bytes=64)
+        nc.sync.dma_start(grows_raw[:], grows.rearrange("(p r) e -> p r e", r=PACK))
+        old_tiles = old.rearrange("(k p) t -> p k t", p=P)
+        old_turn = []
+        for h in range(2):
+            raw = sb.tile([P, 3, HALF_T], F32, name=f"old_turn{h}", tag=("slot_q0", "slot_b")[h], align_bytes=64)
+            nc.sync.dma_start(raw[:], old_tiles[:, 1:4, h * HALF_T : (h + 1) * HALF_T])
+            old_turn.append(raw)
+        old_first = sb.tile([P, T], F32, name="old_first", tag="slot_q1", align_bytes=64)
+        nc.sync.dma_start(old_first[:], old[0:P, :])
+
+        scores = []
+        for r in range(PACK):
+            codes = sb.tile([P, P], U32, name=f"query_codes{r}", align_bytes=64)
+            scales = sb.tile([P, P], U8, name=f"query_scales{r}", align_bytes=64)
+            nc.vector.quantize_mx(out=codes[:].bitcast(FP8X4), scales=scales[:],
+                                  in_=query_bf[:, r].rearrange("p s t -> p (s t)"))
+            score = bank(f"score{r}", f"score{r}")
+            nc.tensor.matmul_mx(out=score[:, 0:I], lhsT=codes[:].bitcast(FP8X4), lhsT_scale=scales[:],
+                                rhs=key_words[:].bitcast(FP4X4), rhs_scale=key_scales[:], start=True, stop=True)
+            scores.append(score)
+
+        fade_turned = bank("stage0", "fade_turned")
+        nc.tensor.transpose(fade_turned[:, 0:P], fade_rows[:], ident[:])
+        fade_cols = sb.tile([P, 8], F32, name="fade_cols")
+        nc.scalar.activation(fade_cols[:], fade_turned[:, 0:8], ACT.Copy)
+        fade_all = sb.tile([P, T], F32, name="fade_all")
+        for h in range(2):
+            spread = bank(f"grad{h}", f"fade_spread{h}")
+            for j in range(4):
+                c = 4 * h + j
+                nc.tensor.transpose(spread[:, j * P : (j + 1) * P], fade_cols[:, c : c + 1].to_broadcast([P, P]), ident[:])
+            nc.scalar.copy(fade_all[:, h * HALF_T : (h + 1) * HALF_T], spread[:])
+
+        inv_sd, neg_inv_sd = [], []
+        for pair in range(2):
+            stats = sb.tile([P, 2, 6], F32, name=f"stats{pair}")
+            moments = sb.tile([P, 2, 2], F32, name=f"moments{pair}")
+            for j in range(2):
+                nc.vector.bn_stats(stats[:, j, :], scores[2 * pair + j][:, 0:I])
+            for j in range(2):
+                nc.vector.bn_aggr(moments[:, j, :], stats[:, j, :])
+            padded = sb.tile([P, 2], F32, name=f"padded{pair}")
+            nc.vector.tensor_scalar(padded[:], moments[:, :, 1], EPS, None, ALU.add)
+            inv = sb.tile([P, 2], F32, name=f"inv_sd{pair}")
+            nc.gpsimd.tensor_tensor(inv[:], padded[:], minus_half[:], ALU.pow)
+            neg = sb.tile([P, 2], F32, name=f"neg_inv_sd{pair}")
+            nc.scalar.activation(neg[:], inv[:], ACT.Copy, scale=-1.0)
+            inv_sd.append(inv)
+            neg_inv_sd.append(neg)
+
+        weights = sb.tile([P, PACK, I], F32, name="weights", tag="weights_then_faded")
+        for r in range(PACK):
+            pair, j = divmod(r, 2)
+            sharpened = sb.tile([P, 2 * I], F32, name="sharpened3", tag="late_cast", align_bytes=64)[:, 0:I] if r == 3 else sb.tile([P, I], F32, name=f"sharpened{r}")[:]
+            top = sb.tile([P, 1], F32, name=f"top{r}")
+            nc.vector.tensor_scalar(sharpened, scores[r][:, 0:I], sharp_sb[:, r : r + 1], None,
+                                    ALU.mult, ALU.max, accum_out=top[:])
+            shift = sb.tile([P, 1], F32, name=f"shift{r}")
+            nc.scalar.activation(shift[:], top[:], ACT.Copy, scale=neg_inv_sd[pair][:, j : j + 1])
+            probs = sb.tile([P, I], F32, name=f"probs{r}")
+            total = sb.tile([P, 1], F32, name=f"total{r}")
+            nc.scalar.activation(probs[:], sharpened, ACT.Exp, bias=shift[:], scale=inv_sd[pair][:, j : j + 1],
+                                 accum_out=total[:])
+            inv_total = sb.tile([P, 1], F32, name=f"inv_total{r}")
+            nc.vector.reciprocal(inv_total[:], total[:])
+            nc.vector.tensor_scalar(weights[:, r, :], probs[:], inv_total[:], qs_sb[:, r : r + 1], ALU.mult, ALU.mult)
+
+        late = sb.tile([P, 2, P, PACK], BF16, name="grows_bf_late", tag="late_cast", align_bytes=64)
+        grows_q = []
+        for k in range(4):
+            grouped = late[:, k - 2] if k >= 2 else sb.tile([P, P, PACK], BF16, name=f"grows_bf{k}", align_bytes=64)[:]
+            nc.scalar.copy(grouped.rearrange("p (c i) r -> p c r i", i=4),
+                           grows_raw[:, :, k * P : (k + 1) * P].rearrange("p r (c i) -> p c r i", i=4))
+            codes = sb.tile([P, P], U32, name=f"grows_codes{k}", align_bytes=64)
+            scales = sb.tile([P, P], U8, name=f"grows_scales{k}", align_bytes=64)
+            nc.vector.quantize_mx(out=codes[:].bitcast(FP8X4), scales=scales[:],
+                                  in_=grouped.rearrange("p c r -> p (c r)"))
+            grows_q.append((codes, scales))
+
+        grads = sb.tile([P, 4, I], F32, name="grads")
+        weight_codes = sb.tile([P, I], U32, name="weight_codes", align_bytes=64)
+        weight_scales = sb.tile([P, I], U8, name="weight_scales", align_bytes=64)
+
+        def gradient(tag, name, ks, slots):
+            width = slots.stop - slots.start
+            grad = bank(tag, name)
+            for j, k in enumerate(ks):
+                nc.tensor.matmul_mx(out=grad[:, j * width : (j + 1) * width], lhsT=grows_q[k][0][:].bitcast(FP8X4),
+                                    lhsT_scale=grows_q[k][1][:], rhs=weight_codes[:, slots].bitcast(FP8X4),
+                                    rhs_scale=weight_scales[:, slots], start=True, stop=True)
+            nc.scalar.copy(grads[:, ks[0] : ks[0] + 2, slots], grad[:, 0 : 2 * width].rearrange("p (k i) -> p k i", k=2))
+
+        for h in range(2):
+            slots = slice(h * HALF_I, (h + 1) * HALF_I)
+            grouped = sb.tile([P, HALF_I, PACK], BF16, name=f"weights_bf{h}", tag=f"weights_bf{h}", align_bytes=64)
+            nc.vector.tensor_copy(grouped[:].rearrange("p (c i) r -> p c r i", i=4),
+                                  weights[:, :, slots].rearrange("p r (c i) -> p c r i", i=4))
+            nc.vector.quantize_mx(out=weight_codes[:, slots].bitcast(FP8X4), scales=weight_scales[:, slots],
+                                  in_=grouped[:].rearrange("p c r -> p (c r)"))
+            gradient(f"score{h}", f"grad_first{h}", (0, 1), slots)
+        gradient("score2", "grad_last", (2, 3), slice(0, I))
+
+        for h in range(2):
+            for k in range(2):
+                nc.vector.tensor_copy(windows[k][:].indirect(offsets[:, 8 * h : 8 * h + 8]), grads[:, k, h * HALF_I : (h + 1) * HALF_I])
+        for k in range(2, 4):
+            nc.vector.tensor_copy(windows[k][:].indirect(offsets[:]), grads[:, k, :])
+
+        faded_first = sb.tile([P, T], F32, name="faded_first", tag="weights_then_faded")
+        for h in range(2):
+            cols = slice(h * HALF_T, (h + 1) * HALF_T)
+            nc.gpsimd.tensor_tensor(faded_first[:, cols], old_first[:, cols], fade_all[:, cols], ALU.mult)
+
+        turned = []
+        for c in range(8):
+            h, j = divmod(c, 4)
+            stage = bank(f"score{(c + 3) % 4}", f"old_turned{c}")
+            for kk in range(3):
+                nc.tensor.transpose(stage[:, kk * P : (kk + 1) * P], old_turn[h][:, kk, j * P : (j + 1) * P], ident[:])
+            faded = sb.tile([P, 3 * P], F32, name=f"faded_turned{c}", tag="weights_bf0" if c == 0 else f"faded_turned{c}", align_bytes=64)
+            nc.scalar.activation(faded[:], stage[:, 0 : 3 * P], ACT.Copy, scale=fade_cols[:, c : c + 1])
+            turned.append(faded)
+
+        def turn_back(k, h, tag):
+            back = bank(tag, f"back{k}_{h}")
+            for j in range(4):
+                nc.tensor.transpose(back[:, j * P : (j + 1) * P], turned[4 * h + j][:, (k - 1) * P : k * P], ident[:])
+            return back
+
+        for k in range(4):
+            for h in range(2):
+                cols = slice(h * HALF_T, (h + 1) * HALF_T)
+                result = sb.tile([P, HALF_T], F32, name=f"result{k}_{h}")
+                if k == 0:
+                    nc.gpsimd.tensor_tensor(result[:], faded_first[:, cols], windows[k][:, cols], ALU.add)
+                elif k == 1:
+                    back = turn_back(k, h, ("stage1", "score3")[h])
+                    faded = sb.tile([P, HALF_T], F32, name=f"faded_second{h}")
+                    nc.scalar.copy(faded[:], back[:])
+                    nc.gpsimd.tensor_tensor(result[:], faded[:], windows[k][:, cols], ALU.add)
+                else:
+                    back = turn_back(k, h, ("grad", "stage")[k - 2] + str(h))
+                    nc.vector.tensor_tensor(result[:], back[:], windows[k][:, cols], ALU.add)
+                nc.sync.dma_start(out[k * P : (k + 1) * P, cols], result[:])

@@ -84,11 +84,9 @@ def tile_attend_bstandardised_v_kernel(tc, query, keys_words, keys_scales, sharp
         old_tiles = old.rearrange("(k p) t -> p k t", p=P)
         old_turn = []
         for h in range(2):
-            raw = sb.tile([P, 3, HALF_T], F32, name=f"old_turn{h}", tag=("slot_q0", "slot_b")[h], align_bytes=64)
-            nc.sync.dma_start(raw[:], old_tiles[:, 1:4, h * HALF_T : (h + 1) * HALF_T])
+            raw = sb.tile([P, 4, HALF_T], F32, name=f"old_turn{h}", tag=("slot_q0", "slot_b")[h], align_bytes=64)
+            nc.sync.dma_start(raw[:], old_tiles[:, :, h * HALF_T : (h + 1) * HALF_T])
             old_turn.append(raw)
-        old_first = sb.tile([P, T], F32, name="old_first", tag="slot_q1", align_bytes=64)
-        nc.sync.dma_start(old_first[:], old[0:P, :])
 
         scores = []
         for r in range(PACK):
@@ -105,13 +103,6 @@ def tile_attend_bstandardised_v_kernel(tc, query, keys_words, keys_scales, sharp
         nc.tensor.transpose(fade_turned[:, 0:P], fade_rows[:], ident[:])
         fade_cols = sb.tile([P, 8], F32, name="fade_cols")
         nc.scalar.activation(fade_cols[:], fade_turned[:, 0:8], ACT.Copy)
-        fade_all = sb.tile([P, T], F32, name="fade_all")
-        for h in range(2):
-            spread = bank(f"grad{h}", f"fade_spread{h}")
-            for j in range(4):
-                c = 4 * h + j
-                nc.tensor.transpose(spread[:, j * P : (j + 1) * P], fade_cols[:, c : c + 1].to_broadcast([P, P]), ident[:])
-            nc.scalar.copy(fade_all[:, h * HALF_T : (h + 1) * HALF_T], spread[:])
 
         inv_sd, neg_inv_sd = [], []
         for pair in range(2):
@@ -130,7 +121,7 @@ def tile_attend_bstandardised_v_kernel(tc, query, keys_words, keys_scales, sharp
             inv_sd.append(inv)
             neg_inv_sd.append(neg)
 
-        weights = sb.tile([P, PACK, I], F32, name="weights", tag="weights_then_faded")
+        weights = sb.tile([P, PACK, I], F32, name="weights")
         for r in range(PACK):
             pair, j = divmod(r, 2)
             sharpened = sb.tile([P, 2 * I], F32, name="sharpened3", tag="late_cast", align_bytes=64)[:, 0:I] if r == 3 else sb.tile([P, I], F32, name=f"sharpened{r}")[:]
@@ -153,7 +144,7 @@ def tile_attend_bstandardised_v_kernel(tc, query, keys_words, keys_scales, sharp
             grouped = late[:, k - 2] if k >= 2 else sb.tile([P, P, PACK], BF16, name=f"grows_bf{k}", align_bytes=64)[:]
             nc.scalar.copy(grouped.rearrange("p (c i) r -> p c r i", i=4),
                            grows_raw[:, :, k * P : (k + 1) * P].rearrange("p r (c i) -> p c r i", i=4))
-            codes = sb.tile([P, P], U32, name=f"grows_codes{k}", align_bytes=64)
+            codes = sb.tile([P, P], U32, name=f"grows_codes{k}", tag=f"grows_codes{k}", align_bytes=64)
             scales = sb.tile([P, P], U8, name=f"grows_scales{k}", align_bytes=64)
             nc.vector.quantize_mx(out=codes[:].bitcast(FP8X4), scales=scales[:],
                                   in_=grouped.rearrange("p c r -> p (c r)"))
@@ -188,39 +179,24 @@ def tile_attend_bstandardised_v_kernel(tc, query, keys_words, keys_scales, sharp
         for k in range(2, 4):
             nc.vector.tensor_copy(windows[k][:].indirect(offsets[:]), grads[:, k, :])
 
-        faded_first = sb.tile([P, T], F32, name="faded_first", tag="weights_then_faded")
-        for h in range(2):
-            cols = slice(h * HALF_T, (h + 1) * HALF_T)
-            nc.gpsimd.tensor_tensor(faded_first[:, cols], old_first[:, cols], fade_all[:, cols], ALU.mult)
-
+        spare = ("grad0", "grad1", "stage1", "stage0", "score3", "score0", "score1", "score2")
+        holds = ("weights_bf0", "grows_codes0", "grows_codes2", "grows_codes3")
         turned = []
         for c in range(8):
             h, j = divmod(c, 4)
-            stage = bank(f"score{(c + 3) % 4}", f"old_turned{c}")
-            for kk in range(3):
-                nc.tensor.transpose(stage[:, kk * P : (kk + 1) * P], old_turn[h][:, kk, j * P : (j + 1) * P], ident[:])
-            faded = sb.tile([P, 3 * P], F32, name=f"faded_turned{c}", tag="weights_bf0" if c == 0 else f"faded_turned{c}", align_bytes=64)
-            nc.scalar.activation(faded[:], stage[:, 0 : 3 * P], ACT.Copy, scale=fade_cols[:, c : c + 1])
+            stage = bank(spare[c], f"old_turned{c}")
+            for k in range(4):
+                nc.tensor.transpose(stage[:, k * P : (k + 1) * P], old_turn[h][:, k, j * P : (j + 1) * P], ident[:])
+            faded = sb.tile([P, E], F32, name=f"faded_turned{c}", tag=holds[c] if c < 4 else f"faded_turned{c}", align_bytes=64)
+            nc.scalar.activation(faded[:], stage[:], ACT.Copy, scale=fade_cols[:, c : c + 1])
             turned.append(faded)
 
-        def turn_back(k, h, tag):
-            back = bank(tag, f"back{k}_{h}")
-            for j in range(4):
-                nc.tensor.transpose(back[:, j * P : (j + 1) * P], turned[4 * h + j][:, (k - 1) * P : k * P], ident[:])
-            return back
-
-        for k in range(4):
-            for h in range(2):
-                cols = slice(h * HALF_T, (h + 1) * HALF_T)
+        for h in range(2):
+            cols = slice(h * HALF_T, (h + 1) * HALF_T)
+            for k in range(4):
+                back = bank(spare[4 * h + k], f"back{k}_{h}")
+                for j in range(4):
+                    nc.tensor.transpose(back[:, j * P : (j + 1) * P], turned[4 * h + j][:, k * P : (k + 1) * P], ident[:])
                 result = sb.tile([P, HALF_T], F32, name=f"result{k}_{h}")
-                if k == 0:
-                    nc.gpsimd.tensor_tensor(result[:], faded_first[:, cols], windows[k][:, cols], ALU.add)
-                elif k == 1:
-                    back = turn_back(k, h, ("stage1", "score3")[h])
-                    faded = sb.tile([P, HALF_T], F32, name=f"faded_second{h}")
-                    nc.scalar.copy(faded[:], back[:])
-                    nc.gpsimd.tensor_tensor(result[:], faded[:], windows[k][:, cols], ALU.add)
-                else:
-                    back = turn_back(k, h, ("grad", "stage")[k - 2] + str(h))
-                    nc.vector.tensor_tensor(result[:], back[:], windows[k][:, cols], ALU.add)
+                nc.vector.tensor_tensor(result[:], back[:], windows[k][:, cols], ALU.add)
                 nc.sync.dma_start(out[k * P : (k + 1) * P, cols], result[:])

@@ -30,13 +30,17 @@ def tile_attend_bstandardised_v_kernel(tc, query, keys_words, keys_scales, sharp
         sb = ctx.enter_context(tc.tile_pool(name="sb", bufs=1))
         ps = ctx.enter_context(tc.psum_pool(name="ps", bufs=1))
 
-        def bank(tag, name):
-            return ps.tile([P, 512], F32, tag=tag, name=name)
+        def bank(number, name):
+            return ps.tile([P, 512], F32, tag=f"bank{number}", name=name)
 
         offsets = sb.tile([P, I // 16], U16, name="offsets")
         nc.sync.dma_start(offsets[:], offs)
         key_scale_pool = sb.tile([P, T], U8, name="key_scale_pool", tag="slot_b", align_bytes=64)
-        nc.gpsimd.memset(key_scale_pool[:].bitcast(I32), 0)
+        nc.vector.memset(key_scale_pool[:].bitcast(I32), 0)
+        zero = sb.tile([P, 2], F32, name="zero", tag="slot_q1", align_bytes=64)
+        nc.vector.memset(zero[:], 0.0)
+        minus_half = sb.tile([P, 2], F32, name="minus_half")
+        nc.vector.tensor_scalar(minus_half[:], zero[:], -0.5, None, ALU.add)
         for quad in range(4):
             nc.scalar.dma_start(key_scale_pool[32 * quad : 32 * quad + 4, :].bitcast(I32),
                                 keys_scales[0, 4 * quad : 4 * quad + 4, :].bitcast(I32))
@@ -55,13 +59,11 @@ def tile_attend_bstandardised_v_kernel(tc, query, keys_words, keys_scales, sharp
         nc.gpsimd.dma_start(sharp_sb[:], sharp.rearrange("(p r) o -> p (r o)", r=PACK))
         qs_sb = sb.tile([P, PACK], F32, name="qs_sb")
         nc.gpsimd.dma_start(qs_sb[:], qs.rearrange("(p r) o -> p (r o)", r=PACK))
-        minus_half = sb.tile([P, 2], F32, name="minus_half")
-        nc.gpsimd.memset(minus_half[:], -0.5)
 
         windows = []
         for k in range(4):
             window = sb.tile([P, T], F32, name=f"window{k}")
-            nc.vector.memset(window[:].bitcast(I32), 0)
+            (nc.vector if k < 2 else nc.gpsimd).memset(window[:].bitcast(I32), 0)
             windows.append(window)
             if k == 1:
                 fade_rows = sb.tile([P, P], F32, name="fade_rows")
@@ -82,86 +84,91 @@ def tile_attend_bstandardised_v_kernel(tc, query, keys_words, keys_scales, sharp
         grows_raw = sb.tile([P, PACK, E], F32, name="grows_raw", tag="slot_a", align_bytes=64)
         nc.sync.dma_start(grows_raw[:], grows.rearrange("(p r) e -> p r e", r=PACK))
         old_tiles = old.rearrange("(k p) t -> p k t", p=P)
-        old_turn = []
-        for h in range(2):
-            raw = sb.tile([P, 4, HALF_T], F32, name=f"old_turn{h}", tag=("slot_q0", "slot_b")[h], align_bytes=64)
-            nc.sync.dma_start(raw[:], old_tiles[:, :, h * HALF_T : (h + 1) * HALF_T])
-            old_turn.append(raw)
+        old_left = sb.tile([P, 3, HALF_T], F32, name="old_left", tag="slot_q0", align_bytes=64)
+        nc.sync.dma_start(old_left[:], old_tiles[:, 1:4, 0:HALF_T])
+        old_first = sb.tile([P, T], F32, name="old_first", tag="slot_b", align_bytes=64)
+        nc.sync.dma_start(old_first[:], old[0:P, :])
+        old_right = sb.tile([P, 3, HALF_T], F32, name="old_right", tag="slot_q1", align_bytes=64)
+        nc.sync.dma_start(old_right[:], old_tiles[:, 1:4, HALF_T:T])
 
         scores = []
-        for r in range(PACK):
-            codes = sb.tile([P, P], U32, name=f"query_codes{r}", align_bytes=64)
-            scales = sb.tile([P, P], U8, name=f"query_scales{r}", align_bytes=64)
+        for pair in range(2):
+            codes = sb.tile([P, 2 * P], U32, name=f"query_codes{pair}", align_bytes=64)
+            scales = sb.tile([P, 2 * P], U8, name=f"query_scales{pair}", align_bytes=64)
             nc.vector.quantize_mx(out=codes[:].bitcast(FP8X4), scales=scales[:],
-                                  in_=query_bf[:, r].rearrange("p s t -> p (s t)"))
-            score = bank(f"score{r}", f"score{r}")
-            nc.tensor.matmul_mx(out=score[:, 0:I], lhsT=codes[:].bitcast(FP8X4), lhsT_scale=scales[:],
-                                rhs=key_words[:].bitcast(FP4X4), rhs_scale=key_scales[:], start=True, stop=True)
+                                  in_=query_bf[:, 2 * pair : 2 * pair + 2].rearrange("p r s t -> p (r s t)"))
+            score = bank(pair, f"score{pair}")
+            for j in range(2):
+                nc.tensor.matmul_mx(out=score[:, j * I : (j + 1) * I], lhsT=codes[:, j * P : (j + 1) * P].bitcast(FP8X4),
+                                    lhsT_scale=scales[:, j * P : (j + 1) * P], rhs=key_words[:].bitcast(FP4X4),
+                                    rhs_scale=key_scales[:], start=True, stop=True)
             scores.append(score)
 
-        fade_turned = bank("stage0", "fade_turned")
+        fade_turned = bank(2, "fade_turned")
         nc.tensor.transpose(fade_turned[:, 0:P], fade_rows[:], ident[:])
         fade_cols = sb.tile([P, 8], F32, name="fade_cols")
-        nc.scalar.activation(fade_cols[:], fade_turned[:, 0:8], ACT.Copy)
+        nc.vector.tensor_copy(fade_cols[:], fade_turned[:, 0:8])
 
-        inv_sd, neg_inv_sd = [], []
+        inv_sd = []
         for pair in range(2):
-            stats = sb.tile([P, 2, 6], F32, name=f"stats{pair}")
-            moments = sb.tile([P, 2, 2], F32, name=f"moments{pair}")
-            for j in range(2):
-                nc.vector.bn_stats(stats[:, j, :], scores[2 * pair + j][:, 0:I])
-            for j in range(2):
-                nc.vector.bn_aggr(moments[:, j, :], stats[:, j, :])
+            stats = sb.tile([P, 2, 3], F32, name=f"stats{pair}")
+            nc.vector.bn_stats(stats[:].rearrange("p j x -> p (j x)"), scores[pair][:].rearrange("p (j i) -> p i j", j=2))
             padded = sb.tile([P, 2], F32, name=f"padded{pair}")
-            nc.vector.tensor_scalar(padded[:], moments[:, :, 1], EPS, None, ALU.add)
+            (nc.gpsimd, nc.vector)[pair].tensor_scalar(padded[:], stats[:, :, 2], 1.0 / I, EPS, ALU.mult, ALU.add)
             inv = sb.tile([P, 2], F32, name=f"inv_sd{pair}")
             nc.gpsimd.tensor_tensor(inv[:], padded[:], minus_half[:], ALU.pow)
-            neg = sb.tile([P, 2], F32, name=f"neg_inv_sd{pair}")
-            nc.scalar.activation(neg[:], inv[:], ACT.Copy, scale=-1.0)
             inv_sd.append(inv)
-            neg_inv_sd.append(neg)
 
         weights = sb.tile([P, PACK, I], F32, name="weights")
-        for r in range(PACK):
-            pair, j = divmod(r, 2)
-            sharpened = sb.tile([P, 2 * I], F32, name="sharpened3", tag="late_cast", align_bytes=64)[:, 0:I] if r == 3 else sb.tile([P, I], F32, name=f"sharpened{r}")[:]
-            top = sb.tile([P, 1], F32, name=f"top{r}")
-            nc.vector.tensor_scalar(sharpened, scores[r][:, 0:I], sharp_sb[:, r : r + 1], None,
-                                    ALU.mult, ALU.max, accum_out=top[:])
-            shift = sb.tile([P, 1], F32, name=f"shift{r}")
-            nc.scalar.activation(shift[:], top[:], ACT.Copy, scale=neg_inv_sd[pair][:, j : j + 1])
-            probs = sb.tile([P, I], F32, name=f"probs{r}")
-            total = sb.tile([P, 1], F32, name=f"total{r}")
-            nc.scalar.activation(probs[:], sharpened, ACT.Exp, bias=shift[:], scale=inv_sd[pair][:, j : j + 1],
-                                 accum_out=total[:])
-            inv_total = sb.tile([P, 1], F32, name=f"inv_total{r}")
-            nc.vector.reciprocal(inv_total[:], total[:])
-            nc.vector.tensor_scalar(weights[:, r, :], probs[:], inv_total[:], qs_sb[:, r : r + 1], ALU.mult, ALU.mult)
+        for pair in range(2):
+            sharpened = sb.tile([P, 2, I], F32, name=f"sharpened{pair}", tag=f"sharpened{pair}", align_bytes=64)
+            top = sb.tile([P, 2], F32, name=f"top{pair}")
+            for j in range(2):
+                r = 2 * pair + j
+                nc.vector.tensor_scalar(sharpened[:, j, :], scores[pair][:, j * I : (j + 1) * I], sharp_sb[:, r : r + 1],
+                                        None, ALU.mult, ALU.max, accum_out=top[:, j : j + 1])
+            shift = sb.tile([P, 2], F32, name=f"shift{pair}", tag=f"probs_in{2 * pair + 1}", align_bytes=64)
+            nc.vector.scalar_tensor_tensor(shift[:], top[:], -1.0, inv_sd[pair][:], ALU.mult, ALU.mult)
+            for j in range(2):
+                r = 2 * pair + j
+                probs = sb.tile([P, I], F32, name=f"probs{r}")
+                total = sb.tile([P, 1], F32, name=f"total{r}")
+                nc.scalar.activation(probs[:], sharpened[:, j, :], ACT.Exp, bias=shift[:, j : j + 1],
+                                     scale=inv_sd[pair][:, j : j + 1], accum_out=total[:])
+                inv_total = sb.tile([P, 1], F32, name=f"inv_total{r}")
+                nc.vector.reciprocal(inv_total[:], total[:])
+                nc.vector.tensor_scalar(weights[:, r, :], probs[:], inv_total[:], qs_sb[:, r : r + 1], ALU.mult, ALU.mult)
 
-        late = sb.tile([P, 2, P, PACK], BF16, name="grows_bf_late", tag="late_cast", align_bytes=64)
         grows_q = []
-        for k in range(4):
-            grouped = late[:, k - 2] if k >= 2 else sb.tile([P, P, PACK], BF16, name=f"grows_bf{k}", align_bytes=64)[:]
-            nc.scalar.copy(grouped.rearrange("p (c i) r -> p c r i", i=4),
-                           grows_raw[:, :, k * P : (k + 1) * P].rearrange("p r (c i) -> p c r i", i=4))
-            codes = sb.tile([P, P], U32, name=f"grows_codes{k}", tag=f"grows_codes{k}", align_bytes=64)
-            scales = sb.tile([P, P], U8, name=f"grows_scales{k}", align_bytes=64)
-            nc.vector.quantize_mx(out=codes[:].bitcast(FP8X4), scales=scales[:],
-                                  in_=grouped.rearrange("p c r -> p (c r)"))
+        for pair in range(2):
+            codes = sb.tile([P, 2 * P], U32, name=f"grows_codes{pair}", tag=f"grows_codes{pair}", align_bytes=64)
+            scales = sb.tile([P, 2 * P], U8, name=f"grows_scales{pair}", tag=f"grows_scales{pair}", align_bytes=64)
             grows_q.append((codes, scales))
-
-        grads = sb.tile([P, 4, I], F32, name="grads")
-        weight_codes = sb.tile([P, I], U32, name="weight_codes", align_bytes=64)
-        weight_scales = sb.tile([P, I], U8, name="weight_scales", align_bytes=64)
-
-        def gradient(tag, name, ks, slots):
-            width = slots.stop - slots.start
-            grad = bank(tag, name)
+        for name, tag, ks in (("a", "grows_bf_a", (0, 1)), ("b", "grows_bf_b", (2,)), ("c", "probs_in3", (3,))):
+            grouped = sb.tile([P, len(ks), P, PACK], BF16, name=f"grows_bf_{name}", tag=tag, align_bytes=64)
             for j, k in enumerate(ks):
-                nc.tensor.matmul_mx(out=grad[:, j * width : (j + 1) * width], lhsT=grows_q[k][0][:].bitcast(FP8X4),
-                                    lhsT_scale=grows_q[k][1][:], rhs=weight_codes[:, slots].bitcast(FP8X4),
+                nc.scalar.copy(grouped[:, j].rearrange("p (c i) r -> p c r i", i=4),
+                               grows_raw[:, :, k * P : (k + 1) * P].rearrange("p r (c i) -> p c r i", i=4))
+            codes, scales = grows_q[ks[0] // 2]
+            cols = slice((ks[0] % 2) * P, (ks[-1] % 2 + 1) * P)
+            nc.vector.quantize_mx(out=codes[:, cols].bitcast(FP8X4), scales=scales[:, cols],
+                                  in_=grouped[:].rearrange("p j c r -> p (j c r)"))
+
+        grads = sb.tile([P, 4 * I], F32, name="grads")
+        weight_codes = sb.tile([P, I], U32, name="weight_codes", tag="weight_codes", align_bytes=64)
+        weight_scales = sb.tile([P, I], U8, name="weight_scales", tag="weight_scales", align_bytes=64)
+
+        def gradients(number, first, last):
+            grad = bank(number, f"grad{number}")
+            for k in range(first // I, (last - 1) // I + 1):
+                lo, hi = max(first, k * I), min(last, (k + 1) * I)
+                slots = slice(lo - k * I, hi - k * I)
+                codes, scales = grows_q[k // 2]
+                cols = slice((k % 2) * P, (k % 2 + 1) * P)
+                nc.tensor.matmul_mx(out=grad[:, lo - first : hi - first], lhsT=codes[:, cols].bitcast(FP8X4),
+                                    lhsT_scale=scales[:, cols], rhs=weight_codes[:, slots].bitcast(FP8X4),
                                     rhs_scale=weight_scales[:, slots], start=True, stop=True)
-            nc.scalar.copy(grads[:, ks[0] : ks[0] + 2, slots], grad[:, 0 : 2 * width].rearrange("p (k i) -> p k i", k=2))
+            nc.scalar.copy(grads[:, first:last], grad[:, 0 : last - first])
 
         for h in range(2):
             slots = slice(h * HALF_I, (h + 1) * HALF_I)
@@ -170,33 +177,67 @@ def tile_attend_bstandardised_v_kernel(tc, query, keys_words, keys_scales, sharp
                                   weights[:, :, slots].rearrange("p r (c i) -> p c r i", i=4))
             nc.vector.quantize_mx(out=weight_codes[:, slots].bitcast(FP8X4), scales=weight_scales[:, slots],
                                   in_=grouped[:].rearrange("p c r -> p (c r)"))
-            gradient(f"score{h}", f"grad_first{h}", (0, 1), slots)
-        gradient("score2", "grad_last", (2, 3), slice(0, I))
+            if h == 0:
+                gradients(0, 0, HALF_I)
+        gradients(1, HALF_I, 2 * I)
+        gradients(2, 2 * I, 4 * I)
 
         for h in range(2):
-            for k in range(2):
-                nc.vector.tensor_copy(windows[k][:].indirect(offsets[:, 8 * h : 8 * h + 8]), grads[:, k, h * HALF_I : (h + 1) * HALF_I])
-        for k in range(2, 4):
-            nc.vector.tensor_copy(windows[k][:].indirect(offsets[:]), grads[:, k, :])
+            nc.vector.tensor_copy(windows[0][:].indirect(offsets[:, 8 * h : 8 * h + 8]), grads[:, h * HALF_I : (h + 1) * HALF_I])
+        for k in range(1, 4):
+            nc.vector.tensor_copy(windows[k][:].indirect(offsets[:]), grads[:, k * I : (k + 1) * I])
 
-        spare = ("grad0", "grad1", "stage1", "stage0", "score3", "score0", "score1", "score2")
-        holds = ("weights_bf0", "grows_codes0", "grows_codes2", "grows_codes3")
+        fade_all = sb.tile([P, T], F32, name="fade_all", tag="sharpened1", align_bytes=64)
+        for h in range(2):
+            spread = bank(3 + h, f"fade_spread{h}")
+            for j in range(4):
+                c = 4 * h + j
+                nc.tensor.transpose(spread[:, j * P : (j + 1) * P], fade_cols[:, c : c + 1].to_broadcast([P, P]), ident[:])
+            nc.scalar.copy(fade_all[:, h * HALF_T : (h + 1) * HALF_T], spread[:])
+
+        faded = {}
+        faded_first = sb.tile([P, T], F32, name="faded_first", tag="weights_bf1", align_bytes=64)
+        nc.gpsimd.tensor_tensor(faded_first[:], old_first[:], fade_all[:], ALU.mult)
+        faded[0, 0], faded[0, 1] = faded_first[:, 0:HALF_T], faded_first[:, HALF_T:T]
+        faded_second = sb.tile([P, HALF_T], F32, name="faded_second", tag="weight_codes", align_bytes=64)
+        nc.gpsimd.tensor_tensor(faded_second[:], old_right[:, 0, :], fade_all[:, HALF_T:T], ALU.mult)
+        faded[1, 1] = faded_second[:]
+
+        stage_banks = (5, 6, 7, 3, 4, 0, 1, 2)
+        holds = ("weight_scales", "grows_codes0", "grows_codes1", "grows_scales1")
         turned = []
         for c in range(8):
             h, j = divmod(c, 4)
-            stage = bank(spare[c], f"old_turned{c}")
-            for k in range(4):
-                nc.tensor.transpose(stage[:, k * P : (k + 1) * P], old_turn[h][:, k, j * P : (j + 1) * P], ident[:])
-            faded = sb.tile([P, E], F32, name=f"faded_turned{c}", tag=holds[c] if c < 4 else f"faded_turned{c}", align_bytes=64)
-            nc.scalar.activation(faded[:], stage[:], ACT.Copy, scale=fade_cols[:, c : c + 1])
-            turned.append(faded)
+            first = 1 + h
+            stage = bank(stage_banks[c], f"old_turned{c}")
+            for k in range(first, 4):
+                nc.tensor.transpose(stage[:, (k - first) * P : (k - first + 1) * P],
+                                    (old_left, old_right)[h][:, k - 1, j * P : (j + 1) * P], ident[:])
+            width = (4 - first) * P
+            tile = sb.tile([P, width], F32, name=f"faded_turned{c}", tag=holds[c] if c < 4 else f"faded_turned{c}", align_bytes=64)
+            nc.scalar.activation(tile[:], stage[:, 0:width], ACT.Copy, scale=fade_cols[:, c : c + 1])
+            turned.append(tile)
 
+        number = 0
         for h in range(2):
-            cols = slice(h * HALF_T, (h + 1) * HALF_T)
-            for k in range(4):
-                back = bank(spare[4 * h + k], f"back{k}_{h}")
+            first = 1 + h
+            for k in range(first, 4):
+                back = bank(stage_banks[number], f"back{k}_{h}")
+                number += 1
                 for j in range(4):
-                    nc.tensor.transpose(back[:, j * P : (j + 1) * P], turned[4 * h + j][:, k * P : (k + 1) * P], ident[:])
-                result = sb.tile([P, HALF_T], F32, name=f"result{k}_{h}")
-                nc.vector.tensor_tensor(result[:], back[:], windows[k][:, cols], ALU.add)
+                    nc.tensor.transpose(back[:, j * P : (j + 1) * P],
+                                        turned[4 * h + j][:, (k - first) * P : (k - first + 1) * P], ident[:])
+                faded[k, h] = back[:]
+        copied = sb.tile([P, HALF_T], F32, name="faded_copied")
+        nc.scalar.copy(copied[:], faded[1, 0])
+        faded[1, 0] = copied[:]
+
+        for k, h in ((0, 0), (0, 1), (1, 1), (1, 0), (2, 0), (3, 0), (2, 1), (3, 1)):
+            pieces = 2 if (k, h) == (3, 1) else 1
+            width = HALF_T // pieces
+            for piece in range(pieces):
+                cols = slice(h * HALF_T + piece * width, h * HALF_T + (piece + 1) * width)
+                result = sb.tile([P, width], F32, name=f"result{k}_{h}_{piece}")
+                (nc.gpsimd if k < 2 else nc.vector).tensor_tensor(
+                    result[:], faded[k, h][:, piece * width : (piece + 1) * width], windows[k][:, cols], ALU.add)
                 nc.sync.dma_start(out[k * P : (k + 1) * P, cols], result[:])

@@ -19,6 +19,10 @@ ACT = mybir.ActivationFunctionType
 
 P = 128
 PACK = 4
+BANK = 512
+TILES = E // P
+BLOCKS = T // P
+LIST_COLUMN = 16
 EPS = 0.05
 HALF_T = T // 2
 HALF_I = I // 2
@@ -31,9 +35,15 @@ def tile_attend_bstandardised_v_kernel(tc, query, keys_words, keys_scales, sharp
         ps = ctx.enter_context(tc.psum_pool(name="ps", bufs=1))
 
         def bank(number, name):
-            return ps.tile([P, 512], F32, tag=f"bank{number}", name=name)
+            return ps.tile([P, BANK], F32, tag=f"bank{number}", name=name)
 
-        offsets = sb.tile([P, I // 16], U16, name="offsets")
+        def quantize(codes, scales, grouped):
+            nc.vector.quantize_mx(out=codes.bitcast(FP8X4), scales=scales, in_=grouped)
+
+        def weave(copy, grouped, rows):
+            copy(grouped.rearrange("p (c i) r -> p c r i", i=4), rows.rearrange("p r (c i) -> p c r i", i=4))
+
+        offsets = sb.tile([P, I // LIST_COLUMN], U16, name="offsets")
         nc.sync.dma_start(offsets[:], offs)
         key_scale_pool = sb.tile([P, T], U8, name="key_scale_pool", tag="slot_b", align_bytes=64)
         nc.vector.memset(key_scale_pool[:].bitcast(I32), 0)
@@ -61,42 +71,40 @@ def tile_attend_bstandardised_v_kernel(tc, query, keys_words, keys_scales, sharp
         nc.gpsimd.dma_start(qs_sb[:], qs.rearrange("(p r) o -> p (r o)", r=PACK))
 
         windows = []
-        for k in range(4):
+        for k in range(TILES):
             window = sb.tile([P, T], F32, name=f"window{k}")
-            (nc.vector if k < 2 else nc.gpsimd).memset(window[:].bitcast(I32), 0)
+            nc.vector.memset(window[:].bitcast(I32), 0)
             windows.append(window)
             if k == 1:
                 fade_rows = sb.tile([P, P], F32, name="fade_rows")
                 nc.vector.memset(fade_rows[:], 0.0)
-                nc.scalar.dma_start(fade_rows[0:8, :], fade.rearrange("o (c n) -> (o c) n", n=P))
-
+                nc.scalar.dma_start(fade_rows[0:BLOCKS, :], fade.rearrange("o (c n) -> (o c) n", n=P))
 
         key_words = sb.tile([P, I], U16, name="key_words", align_bytes=64)
         nc.vector.tensor_copy(key_words[:], key_word_pool[:].indirect(offsets[:]))
-
         query_bf = sb.tile([P, PACK, P, PACK], BF16, name="query_bf", align_bytes=64)
         for u in range(2):
-            nc.vector.tensor_copy(query_bf[:, :, u * (P // 2) : (u + 1) * (P // 2), :].rearrange("p r s t -> p s t r"),
-                                  query_raw[u][:].rearrange("p t (s r) -> p s t r", r=PACK))
+            nc.vector.tensor_copy(query_bf[:, :, u * (P // 2) : (u + 1) * (P // 2), :].rearrange("p r s t -> p s r t"),
+                                  query_raw[u][:].rearrange("p t (s r) -> p s r t", r=PACK))
             if u == 0:
                 key_scales = sb.tile([P, I], U8, name="key_scales", align_bytes=64)
                 nc.vector.tensor_copy(key_scales[:], key_scale_pool[:].indirect(offsets[:]))
+
         grows_raw = sb.tile([P, PACK, E], F32, name="grows_raw", tag="slot_a", align_bytes=64)
         nc.sync.dma_start(grows_raw[:], grows.rearrange("(p r) e -> p r e", r=PACK))
         old_tiles = old.rearrange("(k p) t -> p k t", p=P)
-        old_left = sb.tile([P, 3, HALF_T], F32, name="old_left", tag="slot_q0", align_bytes=64)
-        nc.sync.dma_start(old_left[:], old_tiles[:, 1:4, 0:HALF_T])
+        old_left = sb.tile([P, TILES - 1, HALF_T], F32, name="old_left", tag="slot_q0", align_bytes=64)
+        nc.sync.dma_start(old_left[:], old_tiles[:, 1:TILES, 0:HALF_T])
         old_first = sb.tile([P, T], F32, name="old_first", tag="slot_b", align_bytes=64)
         nc.sync.dma_start(old_first[:], old[0:P, :])
-        old_right = sb.tile([P, 3, HALF_T], F32, name="old_right", tag="slot_q1", align_bytes=64)
-        nc.sync.dma_start(old_right[:], old_tiles[:, 1:4, HALF_T:T])
+        old_right = sb.tile([P, TILES - 1, HALF_T], F32, name="old_right", tag="slot_q1", align_bytes=64)
+        nc.sync.dma_start(old_right[:], old_tiles[:, 1:TILES, HALF_T:T])
 
         scores = []
         for pair in range(2):
             codes = sb.tile([P, 2 * P], U32, name=f"query_codes{pair}", align_bytes=64)
             scales = sb.tile([P, 2 * P], U8, name=f"query_scales{pair}", align_bytes=64)
-            nc.vector.quantize_mx(out=codes[:].bitcast(FP8X4), scales=scales[:],
-                                  in_=query_bf[:, 2 * pair : 2 * pair + 2].rearrange("p r s t -> p (r s t)"))
+            quantize(codes[:], scales[:], query_bf[:, 2 * pair : 2 * pair + 2].rearrange("p r s t -> p (r s t)"))
             score = bank(pair, f"score{pair}")
             for j in range(2):
                 nc.tensor.matmul_mx(out=score[:, j * I : (j + 1) * I], lhsT=codes[:, j * P : (j + 1) * P].bitcast(FP8X4),
@@ -106,8 +114,8 @@ def tile_attend_bstandardised_v_kernel(tc, query, keys_words, keys_scales, sharp
 
         fade_turned = bank(2, "fade_turned")
         nc.tensor.transpose(fade_turned[:, 0:P], fade_rows[:], ident[:])
-        fade_cols = sb.tile([P, 8], F32, name="fade_cols")
-        nc.vector.tensor_copy(fade_cols[:], fade_turned[:, 0:8])
+        fade_cols = sb.tile([P, BLOCKS], F32, name="fade_cols")
+        nc.vector.tensor_copy(fade_cols[:], fade_turned[:, 0:BLOCKS])
 
         inv_sd = []
         for pair in range(2):
@@ -127,7 +135,7 @@ def tile_attend_bstandardised_v_kernel(tc, query, keys_words, keys_scales, sharp
                 r = 2 * pair + j
                 nc.vector.tensor_scalar(sharpened[:, j, :], scores[pair][:, j * I : (j + 1) * I], sharp_sb[:, r : r + 1],
                                         None, ALU.mult, ALU.max, accum_out=top[:, j : j + 1])
-            shift = sb.tile([P, 2], F32, name=f"shift{pair}", tag=f"probs_in{2 * pair + 1}", align_bytes=64)
+            shift = sb.tile([P, 2], F32, name=f"shift{pair}", tag=f"shift{pair}", align_bytes=64)
             nc.vector.scalar_tensor_tensor(shift[:], top[:], -1.0, inv_sd[pair][:], ALU.mult, ALU.mult)
             for j in range(2):
                 r = 2 * pair + j
@@ -144,17 +152,15 @@ def tile_attend_bstandardised_v_kernel(tc, query, keys_words, keys_scales, sharp
             codes = sb.tile([P, 2 * P], U32, name=f"grows_codes{pair}", tag=f"grows_codes{pair}", align_bytes=64)
             scales = sb.tile([P, 2 * P], U8, name=f"grows_scales{pair}", tag=f"grows_scales{pair}", align_bytes=64)
             grows_q.append((codes, scales))
-        for name, tag, ks in (("a", "grows_bf_a", (0, 1)), ("b", "grows_bf_b", (2,)), ("c", "probs_in3", (3,))):
+        for name, tag, ks in (("a", "grows_bf_a", (0, 1)), ("b", "grows_bf_b", (2,)), ("c", "shift1", (3,))):
             grouped = sb.tile([P, len(ks), P, PACK], BF16, name=f"grows_bf_{name}", tag=tag, align_bytes=64)
             for j, k in enumerate(ks):
-                nc.scalar.copy(grouped[:, j].rearrange("p (c i) r -> p c r i", i=4),
-                               grows_raw[:, :, k * P : (k + 1) * P].rearrange("p r (c i) -> p c r i", i=4))
+                weave(nc.scalar.copy, grouped[:, j], grows_raw[:, :, k * P : (k + 1) * P])
             codes, scales = grows_q[ks[0] // 2]
             cols = slice((ks[0] % 2) * P, (ks[-1] % 2 + 1) * P)
-            nc.vector.quantize_mx(out=codes[:, cols].bitcast(FP8X4), scales=scales[:, cols],
-                                  in_=grouped[:].rearrange("p j c r -> p (j c r)"))
+            quantize(codes[:, cols], scales[:, cols], grouped[:].rearrange("p j c r -> p (j c r)"))
 
-        grads = sb.tile([P, 4 * I], F32, name="grads")
+        grads = sb.tile([P, TILES * I], F32, name="grads")
         weight_codes = sb.tile([P, I], U32, name="weight_codes", tag="weight_codes", align_bytes=64)
         weight_scales = sb.tile([P, I], U8, name="weight_scales", tag="weight_scales", align_bytes=64)
 
@@ -173,18 +179,18 @@ def tile_attend_bstandardised_v_kernel(tc, query, keys_words, keys_scales, sharp
         for h in range(2):
             slots = slice(h * HALF_I, (h + 1) * HALF_I)
             grouped = sb.tile([P, HALF_I, PACK], BF16, name=f"weights_bf{h}", tag=f"weights_bf{h}", align_bytes=64)
-            nc.vector.tensor_copy(grouped[:].rearrange("p (c i) r -> p c r i", i=4),
-                                  weights[:, :, slots].rearrange("p r (c i) -> p c r i", i=4))
-            nc.vector.quantize_mx(out=weight_codes[:, slots].bitcast(FP8X4), scales=weight_scales[:, slots],
-                                  in_=grouped[:].rearrange("p c r -> p (c r)"))
+            weave(nc.vector.tensor_copy, grouped[:], weights[:, :, slots])
+            quantize(weight_codes[:, slots], weight_scales[:, slots], grouped[:].rearrange("p c r -> p (c r)"))
             if h == 0:
                 gradients(0, 0, HALF_I)
         gradients(1, HALF_I, 2 * I)
-        gradients(2, 2 * I, 4 * I)
+        gradients(2, 2 * I, TILES * I)
 
+        half_list = HALF_I // LIST_COLUMN
         for h in range(2):
-            nc.vector.tensor_copy(windows[0][:].indirect(offsets[:, 8 * h : 8 * h + 8]), grads[:, h * HALF_I : (h + 1) * HALF_I])
-        for k in range(1, 4):
+            nc.vector.tensor_copy(windows[0][:].indirect(offsets[:, h * half_list : (h + 1) * half_list]),
+                                  grads[:, h * HALF_I : (h + 1) * HALF_I])
+        for k in range(1, TILES):
             nc.vector.tensor_copy(windows[k][:].indirect(offsets[:]), grads[:, k * I : (k + 1) * I])
 
         fade_all = sb.tile([P, T], F32, name="fade_all", tag="sharpened1", align_bytes=64)
@@ -204,36 +210,35 @@ def tile_attend_bstandardised_v_kernel(tc, query, keys_words, keys_scales, sharp
         faded[1, 1] = faded_second[:]
 
         stage_banks = (5, 6, 7, 3, 4, 0, 1, 2)
-        holds = ("weight_scales", "grows_codes0", "grows_codes1", "grows_scales1")
+        left_tags = ("weight_scales", "grows_codes0", "grows_codes1", "grows_scales1")
         turned = []
-        for c in range(8):
+        for c in range(BLOCKS):
             h, j = divmod(c, 4)
             first = 1 + h
             stage = bank(stage_banks[c], f"old_turned{c}")
-            for k in range(first, 4):
+            for k in range(first, TILES):
                 nc.tensor.transpose(stage[:, (k - first) * P : (k - first + 1) * P],
                                     (old_left, old_right)[h][:, k - 1, j * P : (j + 1) * P], ident[:])
-            width = (4 - first) * P
-            tile = sb.tile([P, width], F32, name=f"faded_turned{c}", tag=holds[c] if c < 4 else f"faded_turned{c}", align_bytes=64)
-            nc.scalar.activation(tile[:], stage[:, 0:width], ACT.Copy, scale=fade_cols[:, c : c + 1])
-            turned.append(tile)
+            width = (TILES - first) * P
+            scaled = sb.tile([P, width], F32, name=f"faded_turned{c}",
+                             tag=left_tags[j] if h == 0 else f"faded_turned{c}", align_bytes=64)
+            nc.scalar.activation(scaled[:], stage[:, 0:width], ACT.Copy, scale=fade_cols[:, c : c + 1])
+            turned.append(scaled)
 
-        number = 0
-        for h in range(2):
-            first = 1 + h
-            for k in range(first, 4):
-                back = bank(stage_banks[number], f"back{k}_{h}")
-                number += 1
-                for j in range(4):
-                    nc.tensor.transpose(back[:, j * P : (j + 1) * P],
-                                        turned[4 * h + j][:, (k - first) * P : (k - first + 1) * P], ident[:])
-                faded[k, h] = back[:]
+        turned_back = [(k, h) for h in range(2) for k in range(1 + h, TILES)]
+        for number, (k, h) in zip(stage_banks, turned_back):
+            back = bank(number, f"back{k}_{h}")
+            for j in range(4):
+                nc.tensor.transpose(back[:, j * P : (j + 1) * P],
+                                    turned[4 * h + j][:, (k - 1 - h) * P : (k - h) * P], ident[:])
+            faded[k, h] = back[:]
         copied = sb.tile([P, HALF_T], F32, name="faded_copied")
         nc.scalar.copy(copied[:], faded[1, 0])
         faded[1, 0] = copied[:]
 
-        for k, h in ((0, 0), (0, 1), (1, 1), (1, 0), (2, 0), (3, 0), (2, 1), (3, 1)):
-            pieces = 2 if (k, h) == (3, 1) else 1
+        order = ((0, 0), (0, 1), (1, 1), (1, 0), (2, 0), (3, 0), (2, 1), (3, 1))
+        for k, h in order:
+            pieces = 2 if (k, h) == order[-1] else 1
             width = HALF_T // pieces
             for piece in range(pieces):
                 cols = slice(h * HALF_T + piece * width, h * HALF_T + (piece + 1) * width)

from contextlib import ExitStack

import concourse.mybir as mybir
from concourse.masks import make_identity

D, E, T, I, Q = 512, 512, 1024, 256, 512
FLOPS = 2 * D * Q * I + 2 * Q * E * I

F32 = mybir.dt.float32
BF16 = mybir.dt.bfloat16
I32 = mybir.dt.int32
U32 = mybir.dt.uint32
U16 = mybir.dt.uint16
U8 = mybir.dt.uint8
FP8X4 = mybir.dt.float8_e4m3fn_x4
FP4X4 = mybir.dt.float4_e2m1fn_x4
ALU = mybir.AluOpType
ACT = mybir.ActivationFunctionType

P = 128
PACK = 4
BANK = 512
TILES = E // P
BLOCKS = T // P
LIST_COLUMN = 16
EPS = 0.05
HALF_T = T // 2
HALF_I = I // 2


def tile_attend_bstandardised_v_kernel(tc, query, keys_words, keys_scales, sharp, qs, grows, old, fade, offs, out):
    nc = tc.nc
    with ExitStack() as ctx:
        sb = ctx.enter_context(tc.tile_pool(name="sb", bufs=1))
        ps = ctx.enter_context(tc.psum_pool(name="ps", bufs=1))

        def bank(number, name):
            return ps.tile([P, BANK], F32, tag=f"bank{number}", name=name)

        def quantize(codes, scales, grouped):
            nc.vector.quantize_mx(out=codes.bitcast(FP8X4), scales=scales, in_=grouped)

        def weave(copy, grouped, rows):
            copy(grouped.rearrange("p (c i) r -> p c r i", i=4), rows.rearrange("p r (c i) -> p c r i", i=4))

        offsets = sb.tile([P, I // LIST_COLUMN], U16, name="offsets")
        nc.sync.dma_start(offsets[:], offs)
        key_scale_pool = sb.tile([P, T], U8, name="key_scale_pool", tag="slot_b", align_bytes=64)
        nc.vector.memset(key_scale_pool[:].bitcast(I32), 0)
        zero = sb.tile([P, 2], F32, name="zero", tag="slot_q1", align_bytes=64)
        nc.vector.memset(zero[:], 0.0)
        minus_half = sb.tile([P, 2], F32, name="minus_half")
        nc.vector.tensor_scalar(minus_half[:], zero[:], -0.5, None, ALU.add)
        for quad in range(4):
            nc.scalar.dma_start(key_scale_pool[32 * quad : 32 * quad + 4, :].bitcast(I32),
                                keys_scales[0, 4 * quad : 4 * quad + 4, :].bitcast(I32))
        key_word_pool = sb.tile([P, T], U16, name="key_word_pool", tag="slot_a", align_bytes=64)
        nc.sync.dma_start(key_word_pool[:].bitcast(I32), keys_words[0].bitcast(I32))

        query_rows = query.rearrange("(p t) q -> p t q", t=PACK)
        query_raw = []
        for u in range(2):
            raw = sb.tile([P, PACK, Q // 2], F32, name=f"query_raw{u}", tag=f"slot_q{u}", align_bytes=64)
            nc.sync.dma_start(raw[:], query_rows[:, :, u * (Q // 2) : (u + 1) * (Q // 2)])
            query_raw.append(raw)
        ident = sb.tile([P, P], F32, name="ident")
        make_identity(nc, ident[:])
        sharp_sb = sb.tile([P, PACK], F32, name="sharp_sb")
        nc.gpsimd.dma_start(sharp_sb[:], sharp.rearrange("(p r) o -> p (r o)", r=PACK))
        qs_sb = sb.tile([P, PACK], F32, name="qs_sb")
        nc.gpsimd.dma_start(qs_sb[:], qs.rearrange("(p r) o -> p (r o)", r=PACK))

        windows = []
        for k in range(TILES):
            window = sb.tile([P, T], F32, name=f"window{k}")
            nc.vector.memset(window[:].bitcast(I32), 0)
            windows.append(window)
            if k == 1:
                fade_rows = sb.tile([P, P], F32, name="fade_rows")
                nc.vector.memset(fade_rows[:], 0.0)
                nc.scalar.dma_start(fade_rows[0:BLOCKS, :], fade.rearrange("o (c n) -> (o c) n", n=P))

        key_words = sb.tile([P, I], U16, name="key_words", align_bytes=64)
        nc.vector.tensor_copy(key_words[:], key_word_pool[:].indirect(offsets[:]))
        query_bf = sb.tile([P, PACK, P, PACK], BF16, name="query_bf", align_bytes=64)
        for u in range(2):
            nc.vector.tensor_copy(query_bf[:, :, u * (P // 2) : (u + 1) * (P // 2), :].rearrange("p r s t -> p s r t"),
                                  query_raw[u][:].rearrange("p t (s r) -> p s r t", r=PACK))
            if u == 0:
                key_scales = sb.tile([P, I], U8, name="key_scales", align_bytes=64)
                nc.vector.tensor_copy(key_scales[:], key_scale_pool[:].indirect(offsets[:]))

        grows_raw = sb.tile([P, PACK, E], F32, name="grows_raw", tag="slot_a", align_bytes=64)
        nc.sync.dma_start(grows_raw[:], grows.rearrange("(p r) e -> p r e", r=PACK))
        old_tiles = old.rearrange("(k p) t -> p k t", p=P)
        old_left = sb.tile([P, TILES - 1, HALF_T], F32, name="old_left", tag="slot_q0", align_bytes=64)
        nc.sync.dma_start(old_left[:], old_tiles[:, 1:TILES, 0:HALF_T])
        old_first = sb.tile([P, T], F32, name="old_first", tag="slot_b", align_bytes=64)
        nc.sync.dma_start(old_first[:], old[0:P, :])
        old_right = sb.tile([P, TILES - 1, HALF_T], F32, name="old_right", tag="slot_q1", align_bytes=64)
        nc.sync.dma_start(old_right[:], old_tiles[:, 1:TILES, HALF_T:T])

        scores = []
        for pair in range(2):
            codes = sb.tile([P, 2 * P], U32, name=f"query_codes{pair}", align_bytes=64)
            scales = sb.tile([P, 2 * P], U8, name=f"query_scales{pair}", align_bytes=64)
            quantize(codes[:], scales[:], query_bf[:, 2 * pair : 2 * pair + 2].rearrange("p r s t -> p (r s t)"))
            score = bank(pair, f"score{pair}")
            for j in range(2):
                nc.tensor.matmul_mx(out=score[:, j * I : (j + 1) * I], lhsT=codes[:, j * P : (j + 1) * P].bitcast(FP8X4),
                                    lhsT_scale=scales[:, j * P : (j + 1) * P], rhs=key_words[:].bitcast(FP4X4),
                                    rhs_scale=key_scales[:], start=True, stop=True)
            scores.append(score)

        fade_turned = bank(2, "fade_turned")
        nc.tensor.transpose(fade_turned[:, 0:P], fade_rows[:], ident[:])
        fade_cols = sb.tile([P, BLOCKS], F32, name="fade_cols")
        nc.vector.tensor_copy(fade_cols[:], fade_turned[:, 0:BLOCKS])

        inv_sd = []
        for pair in range(2):
            stats = sb.tile([P, 2, 3], F32, name=f"stats{pair}")
            nc.vector.bn_stats(stats[:].rearrange("p j x -> p (j x)"), scores[pair][:].rearrange("p (j i) -> p i j", j=2))
            padded = sb.tile([P, 2], F32, name=f"padded{pair}")
            (nc.gpsimd, nc.vector)[pair].tensor_scalar(padded[:], stats[:, :, 2], 1.0 / I, EPS, ALU.mult, ALU.add)
            inv = sb.tile([P, 2], F32, name=f"inv_sd{pair}")
            nc.gpsimd.tensor_tensor(inv[:], padded[:], minus_half[:], ALU.pow)
            inv_sd.append(inv)

        weights = sb.tile([P, PACK, I], F32, name="weights")
        for pair in range(2):
            sharpened = sb.tile([P, 2, I], F32, name=f"sharpened{pair}", tag=f"sharpened{pair}", align_bytes=64)
            top = sb.tile([P, 2], F32, name=f"top{pair}")
            for j in range(2):
                r = 2 * pair + j
                nc.vector.tensor_scalar(sharpened[:, j, :], scores[pair][:, j * I : (j + 1) * I], sharp_sb[:, r : r + 1],
                                        None, ALU.mult, ALU.max, accum_out=top[:, j : j + 1])
            shift = sb.tile([P, 2], F32, name=f"shift{pair}", tag=f"shift{pair}", align_bytes=64)
            nc.vector.scalar_tensor_tensor(shift[:], top[:], -1.0, inv_sd[pair][:], ALU.mult, ALU.mult)
            for j in range(2):
                r = 2 * pair + j
                probs = sb.tile([P, I], F32, name=f"probs{r}")
                total = sb.tile([P, 1], F32, name=f"total{r}")
                nc.scalar.activation(probs[:], sharpened[:, j, :], ACT.Exp, bias=shift[:, j : j + 1],
                                     scale=inv_sd[pair][:, j : j + 1], accum_out=total[:])
                inv_total = sb.tile([P, 1], F32, name=f"inv_total{r}")
                nc.vector.reciprocal(inv_total[:], total[:])
                nc.vector.tensor_scalar(weights[:, r, :], probs[:], inv_total[:], qs_sb[:, r : r + 1], ALU.mult, ALU.mult)

        grows_q = []
        for pair in range(2):
            codes = sb.tile([P, 2 * P], U32, name=f"grows_codes{pair}", tag=f"grows_codes{pair}", align_bytes=64)
            scales = sb.tile([P, 2 * P], U8, name=f"grows_scales{pair}", tag=f"grows_scales{pair}", align_bytes=64)
            grows_q.append((codes, scales))
        for name, tag, ks in (("a", "grows_bf_a", (0, 1)), ("b", "grows_bf_b", (2,)), ("c", "shift1", (3,))):
            grouped = sb.tile([P, len(ks), P, PACK], BF16, name=f"grows_bf_{name}", tag=tag, align_bytes=64)
            for j, k in enumerate(ks):
                weave(nc.scalar.copy, grouped[:, j], grows_raw[:, :, k * P : (k + 1) * P])
            codes, scales = grows_q[ks[0] // 2]
            cols = slice((ks[0] % 2) * P, (ks[-1] % 2 + 1) * P)
            quantize(codes[:, cols], scales[:, cols], grouped[:].rearrange("p j c r -> p (j c r)"))

        grads = sb.tile([P, TILES * I], F32, name="grads")
        weight_codes = sb.tile([P, I], U32, name="weight_codes", tag="weight_codes", align_bytes=64)
        weight_scales = sb.tile([P, I], U8, name="weight_scales", tag="weight_scales", align_bytes=64)

        def gradients(number, first, last):
            grad = bank(number, f"grad{number}")
            for k in range(first // I, (last - 1) // I + 1):
                lo, hi = max(first, k * I), min(last, (k + 1) * I)
                slots = slice(lo - k * I, hi - k * I)
                codes, scales = grows_q[k // 2]
                cols = slice((k % 2) * P, (k % 2 + 1) * P)
                nc.tensor.matmul_mx(out=grad[:, lo - first : hi - first], lhsT=codes[:, cols].bitcast(FP8X4),
                                    lhsT_scale=scales[:, cols], rhs=weight_codes[:, slots].bitcast(FP8X4),
                                    rhs_scale=weight_scales[:, slots], start=True, stop=True)
            nc.scalar.copy(grads[:, first:last], grad[:, 0 : last - first])

        for h in range(2):
            slots = slice(h * HALF_I, (h + 1) * HALF_I)
            grouped = sb.tile([P, HALF_I, PACK], BF16, name=f"weights_bf{h}", tag=f"weights_bf{h}", align_bytes=64)
            weave(nc.vector.tensor_copy, grouped[:], weights[:, :, slots])
            quantize(weight_codes[:, slots], weight_scales[:, slots], grouped[:].rearrange("p c r -> p (c r)"))
            if h == 0:
                gradients(0, 0, HALF_I)
        gradients(1, HALF_I, 2 * I)
        gradients(2, 2 * I, TILES * I)

        half_list = HALF_I // LIST_COLUMN
        for h in range(2):
            nc.vector.tensor_copy(windows[0][:].indirect(offsets[:, h * half_list : (h + 1) * half_list]),
                                  grads[:, h * HALF_I : (h + 1) * HALF_I])
        for k in range(1, TILES):
            nc.vector.tensor_copy(windows[k][:].indirect(offsets[:]), grads[:, k * I : (k + 1) * I])

        fade_all = sb.tile([P, T], F32, name="fade_all", tag="sharpened1", align_bytes=64)
        for h in range(2):
            spread = bank(3 + h, f"fade_spread{h}")
            for j in range(4):
                c = 4 * h + j
                nc.tensor.transpose(spread[:, j * P : (j + 1) * P], fade_cols[:, c : c + 1].to_broadcast([P, P]), ident[:])
            nc.scalar.copy(fade_all[:, h * HALF_T : (h + 1) * HALF_T], spread[:])

        faded = {}
        faded_first = sb.tile([P, T], F32, name="faded_first", tag="weights_bf1", align_bytes=64)
        nc.gpsimd.tensor_tensor(faded_first[:], old_first[:], fade_all[:], ALU.mult)
        faded[0, 0], faded[0, 1] = faded_first[:, 0:HALF_T], faded_first[:, HALF_T:T]
        faded_second = sb.tile([P, HALF_T], F32, name="faded_second", tag="weight_codes", align_bytes=64)
        nc.gpsimd.tensor_tensor(faded_second[:], old_right[:, 0, :], fade_all[:, HALF_T:T], ALU.mult)
        faded[1, 1] = faded_second[:]

        stage_banks = (5, 6, 7, 3, 4, 0, 1, 2)
        left_tags = ("weight_scales", "grows_codes0", "grows_codes1", "grows_scales1")
        turned = []
        for c in range(BLOCKS):
            h, j = divmod(c, 4)
            first = 1 + h
            stage = bank(stage_banks[c], f"old_turned{c}")
            for k in range(first, TILES):
                nc.tensor.transpose(stage[:, (k - first) * P : (k - first + 1) * P],
                                    (old_left, old_right)[h][:, k - 1, j * P : (j + 1) * P], ident[:])
            width = (TILES - first) * P
            scaled = sb.tile([P, width], F32, name=f"faded_turned{c}",
                             tag=left_tags[j] if h == 0 else f"faded_turned{c}", align_bytes=64)
            nc.scalar.activation(scaled[:], stage[:, 0:width], ACT.Copy, scale=fade_cols[:, c : c + 1])
            turned.append(scaled)

        turned_back = [(k, h) for h in range(2) for k in range(1 + h, TILES)]
        for number, (k, h) in zip(stage_banks, turned_back):
            back = bank(number, f"back{k}_{h}")
            for j in range(4):
                nc.tensor.transpose(back[:, j * P : (j + 1) * P],
                                    turned[4 * h + j][:, (k - 1 - h) * P : (k - h) * P], ident[:])
            faded[k, h] = back[:]
        copied = sb.tile([P, HALF_T], F32, name="faded_copied")
        nc.scalar.copy(copied[:], faded[1, 0])
        faded[1, 0] = copied[:]

        order = ((0, 0), (0, 1), (1, 1), (1, 0), (2, 0), (3, 0), (2, 1), (3, 1))
        for k, h in order:
            pieces = 2 if (k, h) == order[-1] else 1
            width = HALF_T // pieces
            for piece in range(pieces):
                cols = slice(h * HALF_T + piece * width, h * HALF_T + (piece + 1) * width)
                result = sb.tile([P, width], F32, name=f"result{k}_{h}_{piece}")
                (nc.gpsimd if k < 2 else nc.vector).tensor_tensor(
                    result[:], faded[k, h][:, piece * width : (piece + 1) * width], windows[k][:, cols], ALU.add)
                nc.sync.dma_start(out[k * P : (k + 1) * P, cols], result[:])
